import numpy as np
import ml_dtypes


def mxq(x, axis, fmt="e4m3"):
    dtype, down = {"e4m3": (ml_dtypes.float8_e4m3fn, 7), "e5m2": (ml_dtypes.float8_e5m2, 14)}[fmt]
    v = np.moveaxis(np.asarray(x, np.float32).astype(ml_dtypes.bfloat16).astype(np.float64), axis, -1)
    blocks = v.reshape(v.shape[:-1] + (-1, 32))
    amax = np.abs(blocks).max(-1, keepdims=True)
    byte = np.maximum(np.where(amax > 0, np.frexp(amax)[1] - 1 + 127, 0) - down, 1)
    scale = np.exp2(byte - 127.0)
    codes = (blocks / scale).astype(np.float32).astype(dtype).astype(np.float64)
    return np.moveaxis((codes * scale).reshape(v.shape), -1, axis)


WIDE = False


def mx_kscale(k):
    if not WIDE:
        return np.ones(k)
    levels = np.array([10, -10, 5, -5, 0])
    if k % 512:
        return np.exp2(np.random.permutation(np.resize(levels, k // 32))).repeat(32)
    a = np.empty((k // 512, 16))
    for p in range(k // 512):
        a[p, :8] = np.random.permutation(np.resize(levels, 8))
        for g in range(8):
            far = levels[np.abs(levels - a[p, g]) >= 10]
            a[p, g + 8] = far[np.random.randint(len(far))]
    return np.exp2(a.ravel()).repeat(32)


def f64(x):
    return np.asarray(x).astype(np.float64)


def striped(idx):
    return np.tile(idx.reshape(-1, 16).T, (8, 1)).astype(np.uint16)


def unstriped(offs):
    return offs[:16].T.reshape(-1).astype(np.int64)


E2M1 = np.array([0.0, 0.5, 1.0, 1.5, 2.0, 3.0, 4.0, 6.0, -0.0, -0.5, -1.0, -1.5, -2.0, -3.0, -4.0, -6.0])


def pack_weight(w, fmt):
    k, n = w.shape
    w = f64(np.asarray(w, np.float32).astype(ml_dtypes.bfloat16)).reshape(k // 32, 32, n)
    amax = np.abs(w).max(1)
    if fmt == "e4m3":
        byte = np.frexp(amax)[1] - 1 + 127 - 7
    else:
        mant, ex = np.frexp(amax / 6.0)
        byte = np.where(mant > 0.5, ex, ex - 1) + 127
    byte = np.clip(np.where(amax > 0, byte, 1), 1, 254)
    scaled = (w * np.exp2(127.0 - byte)[:, None, :]).reshape(k, n).astype(np.float32)
    by_word = np.ascontiguousarray(scaled.reshape(k // 512, 128, 4, n).transpose(0, 1, 3, 2))
    if fmt == "e4m3":
        words = by_word.astype(ml_dtypes.float8_e4m3fn).view(np.uint8)
    else:
        c = by_word.astype(ml_dtypes.float4_e2m1fn).view(np.uint8) & 0xF
        words = (c[..., 0::2] | (c[..., 1::2] << 4)).reshape(k // 512, 128, 2 * n)
    return np.ascontiguousarray(words), np.ascontiguousarray(byte.astype(np.uint8).reshape(k // 512, 16, n))


def unpack_weight(words, scales, fmt):
    g, _, n = scales.shape
    words = np.ascontiguousarray(words).reshape(g, 128, n, -1)
    if fmt == "e4m3":
        vals = words.view(ml_dtypes.float8_e4m3fn).astype(np.float64)
    else:
        nib = np.empty((g, 128, n, 4), np.uint8)
        nib[..., 0::2] = words & 0xF
        nib[..., 1::2] = words >> 4
        vals = E2M1[nib]
    vals = vals * np.repeat(np.exp2(scales.astype(np.float64) - 127.0), 8, axis=1)[..., None]
    return vals.transpose(0, 1, 3, 2).reshape(g * 512, n)


def gelu(v):
    return 0.5 * v * (1.0 + np.tanh(np.sqrt(2.0 / np.pi) * (v + 0.044715 * v**3)))


def bf(x):
    return np.asarray(x, np.float32).astype(ml_dtypes.bfloat16)


def planes(Y):
    n, m = Y.shape
    b = f64(bf(Y)).reshape(n // 32, 32, m)
    amax = np.abs(b).max(1)
    byte = np.clip(np.where(amax > 0, np.frexp(amax)[1] - 1 + 127 - 7, 1), 1, 254)
    codes = (b * np.exp2(127.0 - byte)[:, None, :]).reshape(n, m).astype(np.float32).astype(ml_dtypes.float8_e4m3fn).view(np.uint8)
    words = codes.reshape(n // 512, 128, 4, m).transpose(0, 1, 3, 2)
    return np.ascontiguousarray(words), np.ascontiguousarray(byte.astype(np.uint8).reshape(n // 512, 16, m))


K, H, N, T, S, T2, P = 512, 1024, 512, 4096, 1024, 2048, 1024

def setup_inputs():
    n = np.random.standard_normal
    s = mx_kscale(K)[:, None]
    u = mx_kscale(H)[:, None]
    tab_words, tab_scales = pack_weight(n((K, T)) * s, "e4m3")
    w2_words, w2_scales = pack_weight(n((K, H)) / np.sqrt(K) / s * u.T, "e2m1")
    w3_words, w3_scales = pack_weight(n((K, H)) / np.sqrt(K) / s, "e4m3")
    return {
        "tab_words": tab_words, "tab_scales": tab_scales,
        "offs": striped(np.random.permutation(T)[:S]),
        "w1": (n((K, H)) / np.sqrt(K) / s * u.T).astype(np.float32),
        "w2_words": w2_words, "w2_scales": w2_scales,
        "w3_words": w3_words, "w3_scales": w3_scales,
        "offs2": striped(np.random.permutation(T2)[:S]),
        "wgs": np.exp(0.3 * n((128, S))).astype(np.float32),
        "offs3": striped(np.random.permutation(T2)[:P]),
        "ceiling": (n((H, P)) * u).astype(np.float32),
        "w4": (n((H, N)) / np.sqrt(H) / u * np.exp(0.8 * n(N))).astype(np.float32),
    }

def reference(tab_words, tab_scales, offs, w1, w2_words, w2_scales, w3_words, w3_scales,
              offs2, wgs, offs3, ceiling, w4):
    v = unpack_weight(tab_words, tab_scales, "e4m3")[:, unstriped(offs)]
    a = mxq(f64(w1), 0, "e4m3").T @ v
    b = unpack_weight(w2_words, w2_scales, "e2m1").T @ v
    c = unpack_weight(w3_words, w3_scales, "e4m3").T @ v
    h = (a + np.maximum(b, 0.0)) / (1.0 + np.abs(c))
    page = np.zeros((H, T2))
    page[:, unstriped(offs2)] = np.tile(f64(wgs), (H // 128, 1)) * h
    x = page[:, unstriped(offs3)]
    z = np.minimum(x, f64(ceiling))
    y = mxq(f64(w4), 0, "e4m3").T @ mxq(z, 0, "e4m3")
    words, scales = planes(y)
    return y, words, scales

@@ -1,0 +1,253 @@
+from contextlib import ExitStack
+
+import concourse.mybir as mybir
+
+K, H, N, T, S, T2, M = 512, 1024, 512, 4096, 1024, 2048, 1024
+FLOPS = 2 * K * H * S * 3 + 2 * H * N * M
+
+F32 = mybir.dt.float32
+BF16 = mybir.dt.bfloat16
+I32 = mybir.dt.int32
+U32 = mybir.dt.uint32
+U16 = mybir.dt.uint16
+U8 = mybir.dt.uint8
+FP8X4 = mybir.dt.float8_e4m3fn_x4
+FP4X4 = mybir.dt.float4_e2m1fn_x4
+ACT = mybir.ActivationFunctionType
+ALU = mybir.AluOpType
+
+P = 128
+PACK = 4
+PASS = P * PACK
+GROUPS = H // PASS
+BANK = 512
+CHUNK = 256
+STRIPE = 16
+
+
+def tile_list_deadlock_risk_scores_kernel(
+    tc, tab_words, tab_scales, offs, w1, w2_words, w2_scales, w3_words, w3_scales,
+    offs2, wgs, offs3, ceiling, w4, out_0, out_1, out_2,
+):
+    nc = tc.nc
+    with ExitStack() as ctx:
+        keep = ctx.enter_context(tc.tile_pool(name="keep", bufs=1))
+        work = ctx.enter_context(tc.tile_pool(name="work", bufs=2))
+        psum = ctx.enter_context(tc.psum_pool(name="psum", bufs=8))
+
+        pick = keep.tile([P, S // STRIPE], U16, name="pick")
+        put = keep.tile([P, S // STRIPE], U16, name="put")
+        fetch = keep.tile([P, M // STRIPE], U16, name="fetch")
+
+        def load_rows(src, cols):
+            raw = work.tile([P, PACK, PASS], F32, name="raw")
+            nc.sync.dma_start(out=raw[:], in_=src.rearrange("(p j) c -> p j c", j=PACK)[:, :, cols])
+            return raw
+
+        def quantise_weight(raw, codes, scales):
+            grouped = work.tile([P, PASS * PACK], BF16, name="grouped", align_bytes=64)
+            nc.scalar.copy(
+                out=grouped[:].rearrange("p (t m j) -> p m j t", t=PACK, j=PACK),
+                in_=raw[:].rearrange("p j (m t) -> p m j t", t=PACK),
+            )
+            nc.vector.quantize_mx(out=codes.bitcast(FP8X4), scales=scales, in_=grouped[:])
+
+        def load_scale_rows(engine, plane, first, src):
+            for q in range(4):
+                engine.dma_start(
+                    out=plane[32 * q + first : 32 * q + first + 4, :].bitcast(I32),
+                    in_=src[0, 4 * q : 4 * q + 4, :].bitcast(I32),
+                )
+
+        tab_s = keep.tile([P, T], U8, name="tab_s")
+        nc.vector.memset(tab_s[:].bitcast(I32), 0)
+        w23_s_raw = keep.tile([P, H], U8, name="w23_s_raw")
+        nc.gpsimd.memset(w23_s_raw[:].bitcast(I32), 0)
+
+        w1_raw = [load_rows(w1, slice(0, PASS))]
+        load_scale_rows(nc.scalar, tab_s, 0, tab_scales)
+        nc.sync.dma_start(out=pick[:], in_=offs)
+        w3_raw = keep.tile([P, H], I32, name="w3_raw")
+        nc.sync.dma_start(out=w3_raw[:], in_=w3_words[0].rearrange("p n t -> p (n t)").bitcast(I32))
+        w2_raw = keep.tile([P, 2 * H], U8, name="w2_raw")
+        nc.sync.dma_start(out=w2_raw[:].bitcast(I32), in_=w2_words[0].bitcast(I32))
+        tab_w = keep.tile([P, T], I32, name="tab_w", tag="big")
+        nc.sync.dma_start(out=tab_w[:], in_=tab_words[0].rearrange("p n t -> p (n t)").bitcast(I32))
+        load_scale_rows(nc.gpsimd, w23_s_raw, 4, w3_scales)
+        load_scale_rows(nc.gpsimd, w23_s_raw, 0, w2_scales)
+
+        wgs_rows = wgs.rearrange("(m t) j -> m t j", t=PACK)
+        wg_first = keep.tile([P, 1, S], F32, name="wg_first")
+        wg_rest = keep.tile([P, PACK - 1, S], F32, name="wg_rest")
+        for q in range(4):
+            nc.sync.dma_start(out=wg_first[32 * q : 32 * q + 32], in_=wgs_rows[:, 0:1, :])
+        nc.sync.dma_start(out=put[:], in_=offs2)
+        nc.sync.dma_start(out=fetch[:], in_=offs3)
+        for q in range(4):
+            nc.sync.dma_start(out=wg_rest[32 * q : 32 * q + 32], in_=wgs_rows[:, 1:PACK, :])
+        wg = [wg_first[:, 0, :]] + [wg_rest[:, t, :] for t in range(PACK - 1)]
+        w1_raw.append(load_rows(w1, slice(PASS, H)))
+
+        warm = keep.tile([P, 8], F32, name="warm")
+        nc.vector.memset(warm[:], 1.0)
+        nc.scalar.activation(out=warm[:], in_=warm[:], func=ACT.Abs_reciprocal_sqrt)
+
+        pages = [keep.tile([P, T2], F32, name="page%d" % i) for i in range(3)]
+        for page in pages:
+            nc.vector.memset(page[:], 0.0)
+
+        w1_c = keep.tile([P, H], U32, name="w1_c", align_bytes=64)
+        w1_s = keep.tile([P, H], U8, name="w1_s", align_bytes=64)
+        quantise_weight(w1_raw[0], w1_c[:, 0:PASS], w1_s[:, 0:PASS])
+        w3_c = keep.tile([P, H], I32, name="w3_c", align_bytes=64)
+        nc.vector.tensor_copy(
+            out=w3_c[:].rearrange("p (g t m) -> p g m t", g=GROUPS, t=PACK),
+            in_=w3_raw[:].rearrange("p (g m t) -> p g m t", g=GROUPS, t=PACK),
+        )
+        w2_c = keep.tile([P, 2 * H], U8, name="w2_c", align_bytes=64)
+        nc.vector.tensor_copy(
+            out=w2_c[:].rearrange("p (g t m b) -> p g m t b", g=GROUPS, t=PACK, b=2),
+            in_=w2_raw[:].rearrange("p (g m t b) -> p g m t b", g=GROUPS, t=PACK, b=2),
+        )
+        w23_s = keep.tile([P, H], U8, name="w23_s", align_bytes=64)
+        nc.vector.tensor_copy(
+            out=w23_s[:].rearrange("p (g t m) -> p g m t", g=GROUPS, t=PACK),
+            in_=w23_s_raw[:].rearrange("p (g m t) -> p g m t", g=GROUPS, t=PACK),
+        )
+
+        v_c, v_s = [], []
+        for half in range(S // BANK):
+            entries = pick[:, half * BANK // STRIPE : (half + 1) * BANK // STRIPE]
+            scales = keep.tile([P, BANK], U8, name="v_s%d" % half, align_bytes=64)
+            nc.vector.tensor_copy(out=scales[:], in_=tab_s[:].indirect(entries))
+            codes = keep.tile([P, BANK], U32, name="v_c%d" % half, align_bytes=64)
+            nc.vector.tensor_copy(out=codes[:], in_=tab_w[:].bitcast(U32).indirect(entries))
+            v_c.append(codes)
+            v_s.append(scales)
+
+        ceil = [
+            keep.tile([P, PACK, M], F32, name="ceil0"),
+            keep.tile([P, PACK, M], F32, name="ceil1", tag="big"),
+        ]
+        w4_c = keep.tile([P, GROUPS * N], U32, name="w4_c", align_bytes=64)
+        w4_s = keep.tile([P, GROUPS * N], U8, name="w4_s", align_bytes=64)
+        x = [keep.tile([P, PACK, M], F32, name="x%d" % g) for g in range(GROUPS)]
+        h = [keep.tile([P, S], F32, name="h%d" % i, align_bytes=64) for i in range(2)]
+
+        def features(s):
+            g, t = divmod(s, PACK)
+            rows = slice(s * P, (s + 1) * P)
+            lin = work.tile([P, S], F32, name="lin", bufs=3)
+            gate = work.tile([P, S], F32, name="gate") if s > 0 else None
+            damp = work.tile([P, S], F32, name="damp", bufs=3)
+            by_halves = s < 3
+            for half in range(S // BANK):
+                cols = slice(half * BANK, (half + 1) * BANK)
+                moving = dict(rhs=v_c[half][:].bitcast(FP8X4), rhs_scale=v_s[half][:], start=True, stop=True)
+                c = psum.tile([P, BANK], F32, name="c", tag="bank")
+                nc.tensor.matmul_mx(out=c[:], lhsT=w3_c[:, rows].bitcast(FP8X4), lhsT_scale=w23_s[4:P, rows], **moving)
+                b = psum.tile([P, BANK], F32, name="b", tag="bank")
+                nc.tensor.matmul_mx(
+                    out=b[:], lhsT=w2_c[:, 2 * s * P : 2 * (s + 1) * P].bitcast(FP4X4), lhsT_scale=w23_s[:, rows], **moving
+                )
+                a = psum.tile([P, BANK], F32, name="a", tag="bank")
+                nc.tensor.matmul_mx(out=a[:], lhsT=w1_c[:, rows].bitcast(FP8X4), lhsT_scale=w1_s[:, rows], **moving)
+                nc.scalar.activation(out=damp[:, cols], in_=c[:], func=ACT.Abs)
+                nc.scalar.copy(out=lin[:, cols], in_=a[:])
+                if s == 0:
+                    nc.vector.scalar_tensor_tensor(
+                        out=lin[:, cols], in0=b[:], scalar=0.0, in1=lin[:, cols], op0=ALU.max, op1=ALU.add
+                    )
+                else:
+                    nc.scalar.activation(out=gate[:, cols], in_=b[:], func=ACT.Relu)
+                if by_halves or half == 1:
+                    cols = cols if by_halves else slice(0, S)
+                    nc.scalar.activation(out=damp[:, cols], in_=damp[:, cols], func=ACT.Abs_reciprocal_sqrt, bias=1.0)
+                    nc.scalar.activation(out=damp[:, cols], in_=damp[:, cols], func=ACT.Square)
+                    engine = nc.vector if s == 0 else nc.gpsimd
+                    if s > 0:
+                        engine.tensor_tensor(out=lin[:, cols], in0=lin[:, cols], in1=gate[:, cols], op=ALU.add)
+                    engine.tensor_tensor(out=damp[:, cols], in0=damp[:, cols], in1=wg[t][:, cols], op=ALU.mult)
+                    engine.tensor_tensor(out=h[s % 2][:, cols], in0=lin[:, cols], in1=damp[:, cols], op=ALU.mult)
+                    entries = put[:, cols.start // STRIPE : cols.stop // STRIPE]
+                    nc.vector.tensor_copy(out=pages[s % 3][:].indirect(entries), in_=h[s % 2][:, cols])
+
+        def fetch_columns(s, cols):
+            g, t = divmod(s, PACK)
+            entries = fetch[:, cols.start // STRIPE : cols.stop // STRIPE]
+            nc.vector.tensor_copy(out=x[g][:, t, cols], in_=pages[s % 3][:].indirect(entries))
+
+        slices = GROUPS * PACK
+        for s in range(slices):
+            features(s)
+            if s >= 1:
+                fetch_columns(s - 1, slice(0, M))
+            if s == 0:
+                quantise_weight(w1_raw[1], w1_c[:, PASS:H], w1_s[:, PASS:H])
+            if s in (1, 2):
+                g = s - 1
+                raw = load_rows(w4[g * PASS : (g + 1) * PASS, :], slice(0, N))
+                quantise_weight(raw, w4_c[:, g * N : (g + 1) * N], w4_s[:, g * N : (g + 1) * N])
+                nc.sync.dma_start(
+                    out=ceil[g][:], in_=ceiling[g * PASS : (g + 1) * PASS, :].rearrange("(p t) m -> p t m", t=PACK)
+                )
+
+        y_c = keep.tile([P, M], I32, name="y_c", align_bytes=64)
+        y_s = keep.tile([P, M], U8, name="y_s", align_bytes=64)
+        y_rows = out_0.rearrange("(p t) m -> p t m", t=PACK)
+        y_words = out_1[0].rearrange("p m t -> p (m t)").bitcast(I32)
+
+        def scores(ch):
+            cols = slice(ch * CHUNK, (ch + 1) * CHUNK)
+            fetch_columns(slices - 1, cols)
+            width = CHUNK * PACK
+            z = [h[1 - g][:].bitcast(BF16)[:, (ch % 2) * width : (ch % 2 + 1) * width] for g in range(GROUPS)]
+            for g in range(GROUPS):
+                nc.vector.tensor_tensor(
+                    out=z[g].rearrange("p (c i t) -> p c t i", i=4, t=PACK),
+                    in0=x[g][:, :, cols].rearrange("p t (c i) -> p c t i", i=4),
+                    in1=ceil[g][:, :, cols].rearrange("p t (c i) -> p c t i", i=4),
+                    op=ALU.min,
+                )
+            z_c, z_s = [], []
+            for g in range(GROUPS):
+                codes = work.tile([P, CHUNK], U32, name="z_c%d" % g, align_bytes=64)
+                scales = work.tile([P, CHUNK], U8, name="z_s%d" % g, align_bytes=64)
+                nc.vector.quantize_mx(out=codes[:].bitcast(FP8X4), scales=scales[:], in_=z[g])
+                z_c.append(codes)
+                z_s.append(scales)
+            y = work.tile([P, PACK, CHUNK], F32, name="y")
+            for pair in range(2):
+                acc = psum.tile([P, 2, CHUNK], F32, name="acc", tag="bank")
+                for u in range(2):
+                    t = 2 * pair + u
+                    for g in range(GROUPS):
+                        wcols = slice(g * N + t * P, g * N + (t + 1) * P)
+                        nc.tensor.matmul_mx(
+                            out=acc[:, u, :], lhsT=w4_c[:, wcols].bitcast(FP8X4), lhsT_scale=w4_s[:, wcols],
+                            rhs=z_c[g][:].bitcast(FP8X4), rhs_scale=z_s[g][:], start=(g == 0), stop=(g == GROUPS - 1),
+                        )
+                nc.scalar.copy(out=y[:, 2 * pair : 2 * pair + 2, :], in_=acc[:])
+            nc.sync.dma_start(out=y_rows[:, :, cols], in_=y[:])
+            y_b = work.tile([P, CHUNK * PACK], BF16, name="y_b", align_bytes=64)
+            nc.scalar.copy(
+                out=y_b[:].rearrange("p (c i t) -> p c t i", i=4, t=PACK),
+                in_=y[:].rearrange("p t (c i) -> p c t i", i=4),
+            )
+            return y_b
+
+        def score_planes(ch, y_b):
+            cols = slice(ch * CHUNK, (ch + 1) * CHUNK)
+            nc.vector.quantize_mx(out=y_c[:, cols].bitcast(FP8X4), scales=y_s[:, cols], in_=y_b[:])
+            nc.sync.dma_start(out=y_words[:, cols], in_=y_c[:, cols])
+
+        rounded = []
+        for ch in range(M // CHUNK):
+            rounded.append(scores(ch))
+            if ch >= 1:
+                score_planes(ch - 1, rounded[ch - 1])
+        score_planes(M // CHUNK - 1, rounded[-1])
+        for q in range(4):
+            nc.sync.dma_start(
+                out=out_2[0, 4 * q : 4 * q + 4, :].bitcast(I32), in_=y_s[32 * q : 32 * q + 4, :].bitcast(I32)
+            )

@@ -33,6 +33,7 @@ def tile_list_deadlock_risk_scores_kernel(
     with ExitStack() as ctx:
         keep = ctx.enter_context(tc.tile_pool(name="keep", bufs=1))
         work = ctx.enter_context(tc.tile_pool(name="work", bufs=2))
+        late = ctx.enter_context(tc.tile_pool(name="late", bufs=1))
         psum = ctx.enter_context(tc.psum_pool(name="psum", bufs=8))
 
         pick = keep.tile([P, S // STRIPE], U16, name="pick")
@@ -40,21 +41,27 @@ def tile_list_deadlock_risk_scores_kernel(
         fetch = keep.tile([P, M // STRIPE], U16, name="fetch")
 
         def load_rows(src, cols):
-            raw = work.tile([P, PACK, PASS], F32, name="raw")
+            raw = work.tile([P, PACK, PASS], F32, name="raw", bufs=3)
             nc.sync.dma_start(out=raw[:], in_=src.rearrange("(p j) c -> p j c", j=PACK)[:, :, cols])
             return raw
 
-        def quantise_weight(raw, codes, scales):
+        def deal_columns(raw):
             grouped = work.tile([P, PASS * PACK], BF16, name="grouped", align_bytes=64)
             nc.scalar.copy(
                 out=grouped[:].rearrange("p (t m j) -> p m j t", t=PACK, j=PACK),
                 in_=raw[:].rearrange("p j (m t) -> p m j t", t=PACK),
             )
-            nc.vector.quantize_mx(out=codes.bitcast(FP8X4), scales=scales, in_=grouped[:])
+            return grouped
 
-        def load_scale_rows(engine, plane, first, src):
-            for q in range(4):
-                engine.dma_start(
+        def quantise(grouped, codes, scales):
+            nc.vector.quantize_mx(out=codes.bitcast(FP8X4), scales=scales, in_=grouped)
+
+        def interleave(copy, out, planes):
+            copy(out=out.rearrange("p (c i t) -> p c t i", i=4, t=PACK), in_=planes.rearrange("p t (c i) -> p c t i", i=4))
+
+        def load_scale_rows(plane, first, src, quadrants):
+            for q in quadrants:
+                nc.sync.dma_start(
                     out=plane[32 * q + first : 32 * q + first + 4, :].bitcast(I32),
                     in_=src[0, 4 * q : 4 * q + 4, :].bitcast(I32),
                 )
@@ -64,51 +71,67 @@ def tile_list_deadlock_risk_scores_kernel(
         w23_s_raw = keep.tile([P, H], U8, name="w23_s_raw")
         nc.gpsimd.memset(w23_s_raw[:].bitcast(I32), 0)
 
-        w1_raw = [load_rows(w1, slice(0, PASS))]
-        load_scale_rows(nc.scalar, tab_s, 0, tab_scales)
         nc.sync.dma_start(out=pick[:], in_=offs)
-        w3_raw = keep.tile([P, H], I32, name="w3_raw")
-        nc.sync.dma_start(out=w3_raw[:], in_=w3_words[0].rearrange("p n t -> p (n t)").bitcast(I32))
-        w2_raw = keep.tile([P, 2 * H], U8, name="w2_raw")
-        nc.sync.dma_start(out=w2_raw[:].bitcast(I32), in_=w2_words[0].bitcast(I32))
-        tab_w = keep.tile([P, T], I32, name="tab_w", tag="big")
-        nc.sync.dma_start(out=tab_w[:], in_=tab_words[0].rearrange("p n t -> p (n t)").bitcast(I32))
-        load_scale_rows(nc.gpsimd, w23_s_raw, 4, w3_scales)
-        load_scale_rows(nc.gpsimd, w23_s_raw, 0, w2_scales)
+        w1_raw = [load_rows(w1, slice(0, PASS))]
+        w3_raw = [keep.tile([P, PASS], I32, name="w3_raw%d" % g) for g in range(GROUPS)]
+        w2_raw = [keep.tile([P, 2 * PASS], U8, name="w2_raw%d" % g) for g in range(GROUPS)]
 
+        def load_words(g):
+            cols = slice(g * PASS, (g + 1) * PASS)
+            nc.sync.dma_start(out=w3_raw[g][:], in_=w3_words[0].rearrange("p n t -> p (n t)").bitcast(I32)[:, cols])
+            cols = slice(g * PASS // 2, (g + 1) * PASS // 2)
+            nc.sync.dma_start(out=w2_raw[g][:].bitcast(I32), in_=w2_words[0].bitcast(I32)[:, cols])
+
+        load_scale_rows(w23_s_raw, 4, w3_scales, range(4))
+        load_scale_rows(w23_s_raw, 0, w2_scales, range(2))
+        load_words(0)
+        load_scale_rows(w23_s_raw, 0, w2_scales, range(2, 4))
+        load_scale_rows(tab_s, 0, tab_scales, range(4))
+        tab_w = keep.tile([P, T], I32, name="tab_w", align_bytes=64)
+        nc.sync.dma_start(out=tab_w[:], in_=tab_words[0].rearrange("p n t -> p (n t)").bitcast(I32))
+
+        load_words(1)
         wgs_rows = wgs.rearrange("(m t) j -> m t j", t=PACK)
-        wg_first = keep.tile([P, 1, S], F32, name="wg_first")
-        wg_rest = keep.tile([P, PACK - 1, S], F32, name="wg_rest")
-        for q in range(4):
-            nc.sync.dma_start(out=wg_first[32 * q : 32 * q + 32], in_=wgs_rows[:, 0:1, :])
-        nc.sync.dma_start(out=put[:], in_=offs2)
-        nc.sync.dma_start(out=fetch[:], in_=offs3)
-        for q in range(4):
-            nc.sync.dma_start(out=wg_rest[32 * q : 32 * q + 32], in_=wgs_rows[:, 1:PACK, :])
-        wg = [wg_first[:, 0, :]] + [wg_rest[:, t, :] for t in range(PACK - 1)]
-        w1_raw.append(load_rows(w1, slice(PASS, H)))
+        wg_tiles = [
+            (keep.tile([P, 1, S], F32, name="wg0"), 0, 1),
+            (keep.tile([P, 1, S], F32, name="wg1"), 1, 2),
+            (late.tile([P, 2, S], F32, name="wg23", align_bytes=64, offset=4 * S), 2, 4),
+        ]
+        wg = []
+        for tile, first, last in wg_tiles:
+            for q in range(4):
+                nc.sync.dma_start(out=tile[32 * q : 32 * q + 32], in_=wgs_rows[:, first:last, :])
+            wg.extend(tile[:, t, :] for t in range(last - first))
+            if first == 0:
+                nc.sync.dma_start(out=put[:], in_=offs2)
+                w1_raw.append(load_rows(w1, slice(PASS, H)))
+                nc.sync.dma_start(out=fetch[:], in_=offs3)
 
         warm = keep.tile([P, 8], F32, name="warm")
         nc.vector.memset(warm[:], 1.0)
         nc.scalar.activation(out=warm[:], in_=warm[:], func=ACT.Abs_reciprocal_sqrt)
 
-        pages = [keep.tile([P, T2], F32, name="page%d" % i) for i in range(3)]
+        pages = [keep.tile([P, T2], F32, name="page%d" % i) for i in range(2)]
         for page in pages:
-            nc.vector.memset(page[:], 0.0)
+            nc.vector.memset(page[:].bitcast(I32), 0)
 
         w1_c = keep.tile([P, H], U32, name="w1_c", align_bytes=64)
         w1_s = keep.tile([P, H], U8, name="w1_s", align_bytes=64)
-        quantise_weight(w1_raw[0], w1_c[:, 0:PASS], w1_s[:, 0:PASS])
+        quantise(deal_columns(w1_raw[0])[:], w1_c[:, 0:PASS], w1_s[:, 0:PASS])
         w3_c = keep.tile([P, H], I32, name="w3_c", align_bytes=64)
-        nc.vector.tensor_copy(
-            out=w3_c[:].rearrange("p (g t m) -> p g m t", g=GROUPS, t=PACK),
-            in_=w3_raw[:].rearrange("p (g m t) -> p g m t", g=GROUPS, t=PACK),
-        )
         w2_c = keep.tile([P, 2 * H], U8, name="w2_c", align_bytes=64)
-        nc.vector.tensor_copy(
-            out=w2_c[:].rearrange("p (g t m b) -> p g m t b", g=GROUPS, t=PACK, b=2),
-            in_=w2_raw[:].rearrange("p (g m t b) -> p g m t b", g=GROUPS, t=PACK, b=2),
-        )
+
+        def deal_words(g):
+            nc.vector.tensor_copy(
+                out=w3_c[:, g * PASS : (g + 1) * PASS].rearrange("p (t m) -> p m t", t=PACK),
+                in_=w3_raw[g][:].rearrange("p (m t) -> p m t", t=PACK),
+            )
+            nc.vector.tensor_copy(
+                out=w2_c[:, 2 * g * PASS : 2 * (g + 1) * PASS].rearrange("p (t m b) -> p m t b", t=PACK, b=2),
+                in_=w2_raw[g][:].rearrange("p (m t b) -> p m t b", t=PACK, b=2),
+            )
+
+        deal_words(0)
         w23_s = keep.tile([P, H], U8, name="w23_s", align_bytes=64)
         nc.vector.tensor_copy(
             out=w23_s[:].rearrange("p (g t m) -> p g m t", g=GROUPS, t=PACK),
@@ -125,13 +148,10 @@ def tile_list_deadlock_risk_scores_kernel(
             v_c.append(codes)
             v_s.append(scales)
 
-        ceil = [
-            keep.tile([P, PACK, M], F32, name="ceil0"),
-            keep.tile([P, PACK, M], F32, name="ceil1", tag="big"),
-        ]
-        w4_c = keep.tile([P, GROUPS * N], U32, name="w4_c", align_bytes=64)
-        w4_s = keep.tile([P, GROUPS * N], U8, name="w4_s", align_bytes=64)
-        x = [keep.tile([P, PACK, M], F32, name="x%d" % g) for g in range(GROUPS)]
+        deal_words(1)
+
+        x = [keep.tile([P, PACK, M], BF16, name="x%d" % g) for g in range(GROUPS)]
+        ceil = [keep.tile([P, M * PACK], BF16, name="ceil%d" % g, align_bytes=64) for g in range(GROUPS)]
         h = [keep.tile([P, S], F32, name="h%d" % i, align_bytes=64) for i in range(2)]
 
         def features(s):
@@ -170,70 +190,92 @@ def tile_list_deadlock_risk_scores_kernel(
                     engine.tensor_tensor(out=damp[:, cols], in0=damp[:, cols], in1=wg[t][:, cols], op=ALU.mult)
                     engine.tensor_tensor(out=h[s % 2][:, cols], in0=lin[:, cols], in1=damp[:, cols], op=ALU.mult)
                     entries = put[:, cols.start // STRIPE : cols.stop // STRIPE]
-                    nc.vector.tensor_copy(out=pages[s % 3][:].indirect(entries), in_=h[s % 2][:, cols])
+                    nc.vector.tensor_copy(out=pages[s % 2][:].indirect(entries), in_=h[s % 2][:, cols])
 
         def fetch_columns(s, cols):
             g, t = divmod(s, PACK)
             entries = fetch[:, cols.start // STRIPE : cols.stop // STRIPE]
-            nc.vector.tensor_copy(out=x[g][:, t, cols], in_=pages[s % 3][:].indirect(entries))
+            nc.vector.tensor_copy(out=x[g][:, t, cols], in_=pages[s % 2][:].indirect(entries))
+
+        def words(ch, width=CHUNK):
+            return slice(ch * width * PACK, (ch + 1) * width * PACK)
 
         slices = GROUPS * PACK
+        w4_grouped = []
         for s in range(slices):
             features(s)
             if s >= 1:
                 fetch_columns(s - 1, slice(0, M))
             if s == 0:
-                quantise_weight(w1_raw[1], w1_c[:, PASS:H], w1_s[:, PASS:H])
-            if s in (1, 2):
-                g = s - 1
-                raw = load_rows(w4[g * PASS : (g + 1) * PASS, :], slice(0, N))
-                quantise_weight(raw, w4_c[:, g * N : (g + 1) * N], w4_s[:, g * N : (g + 1) * N])
-                nc.sync.dma_start(
-                    out=ceil[g][:], in_=ceiling[g * PASS : (g + 1) * PASS, :].rearrange("(p t) m -> p t m", t=PACK)
-                )
+                quantise(deal_columns(w1_raw[1])[:], w1_c[:, PASS:H], w1_s[:, PASS:H])
+        for g in range(GROUPS):
+            w4_grouped.append(deal_columns(load_rows(w4[g * PASS : (g + 1) * PASS, :], slice(0, N))))
+        for g in range(GROUPS):
+            for half in range(M // PASS):
+                raw = load_rows(ceiling[g * PASS : (g + 1) * PASS, :], slice(half * PASS, (half + 1) * PASS))
+                for u in range(PASS // CHUNK):
+                    interleave(nc.scalar.copy, ceil[g][:, words(2 * half + u)], raw[:, :, u * CHUNK : (u + 1) * CHUNK])
+        x_i = [
+            late.tile([P, M * PACK], BF16, name="x_i0", align_bytes=64, offset=0),
+            keep.tile([P, M * PACK], BF16, name="x_i1", tag="tab_w", align_bytes=64),
+        ]
+        for ch in range(M // CHUNK):
+            interleave(nc.scalar.copy, x_i[0][:, words(ch)], x[0][:, :, ch * CHUNK : (ch + 1) * CHUNK])
+        w4_c = late.tile([P, GROUPS * N], U32, name="w4_c", align_bytes=64, offset=2 * M * PACK)
+        w4_s = keep.tile([P, GROUPS * N], U8, name="w4_s", align_bytes=64)
+        for g in range(GROUPS):
+            quantise(w4_grouped[g][:], w4_c[:, g * N : (g + 1) * N], w4_s[:, g * N : (g + 1) * N])
+        for ch in range(M // CHUNK):
+            fetch_columns(slices - 1, slice(ch * CHUNK, (ch + 1) * CHUNK))
+        for ch in range(M // CHUNK):
+            interleave(nc.scalar.copy, x_i[1][:, words(ch)], x[1][:, :, ch * CHUNK : (ch + 1) * CHUNK])
 
         y_c = keep.tile([P, M], I32, name="y_c", align_bytes=64)
         y_s = keep.tile([P, M], U8, name="y_s", align_bytes=64)
         y_rows = out_0.rearrange("(p t) m -> p t m", t=PACK)
         y_words = out_1[0].rearrange("p m t -> p (m t)").bitcast(I32)
 
+        def capped(g, cols, z, name):
+            nc.vector.tensor_tensor(
+                out=z, in0=x_i[g][:, PACK * cols.start : PACK * cols.stop],
+                in1=ceil[g][:, PACK * cols.start : PACK * cols.stop], op=ALU.min,
+            )
+            codes = keep.tile([P, cols.stop - cols.start], U32, name=name + "_c", align_bytes=64)
+            scales = keep.tile([P, cols.stop - cols.start], U8, name=name + "_s", align_bytes=64)
+            quantise(z, codes[:], scales[:])
+            return codes, scales
+
+        def add_pass(acc, pair, g, codes, scales):
+            for u in range(2):
+                t = 2 * pair + u
+                wcols = slice(g * N + t * P, g * N + (t + 1) * P)
+                nc.tensor.matmul_mx(
+                    out=acc[:, u, :], lhsT=w4_c[:, wcols].bitcast(FP8X4), lhsT_scale=w4_s[:, wcols],
+                    rhs=codes.bitcast(FP8X4), rhs_scale=scales, start=(g == 0 and u == 0), stop=(g == 1 and u == 1),
+                )
+
+        acc = []
+
+        def first_pass(half):
+            cols = slice(half * 2 * CHUNK, (half + 1) * 2 * CHUNK)
+            codes, scales = capped(0, cols, h[1][:].bitcast(BF16), "z0%d" % half)
+            for u in range(2):
+                part = slice(u * CHUNK, (u + 1) * CHUNK)
+                banks = [psum.tile([P, 2, CHUNK], F32, name="acc", tag="bank") for pair in range(2)]
+                for pair in range(2):
+                    add_pass(banks[pair], pair, 0, codes[:, part], scales[:, part])
+                acc.append(banks)
+
         def scores(ch):
             cols = slice(ch * CHUNK, (ch + 1) * CHUNK)
-            fetch_columns(slices - 1, cols)
-            width = CHUNK * PACK
-            z = [h[1 - g][:].bitcast(BF16)[:, (ch % 2) * width : (ch % 2 + 1) * width] for g in range(GROUPS)]
-            for g in range(GROUPS):
-                nc.vector.tensor_tensor(
-                    out=z[g].rearrange("p (c i t) -> p c t i", i=4, t=PACK),
-                    in0=x[g][:, :, cols].rearrange("p t (c i) -> p c t i", i=4),
-                    in1=ceil[g][:, :, cols].rearrange("p t (c i) -> p c t i", i=4),
-                    op=ALU.min,
-                )
-            z_c, z_s = [], []
-            for g in range(GROUPS):
-                codes = work.tile([P, CHUNK], U32, name="z_c%d" % g, align_bytes=64)
-                scales = work.tile([P, CHUNK], U8, name="z_s%d" % g, align_bytes=64)
-                nc.vector.quantize_mx(out=codes[:].bitcast(FP8X4), scales=scales[:], in_=z[g])
-                z_c.append(codes)
-                z_s.append(scales)
-            y = work.tile([P, PACK, CHUNK], F32, name="y")
+            codes, scales = capped(1, cols, x_i[1][:, words(ch)], "z1%d" % ch)
+            y = work.tile([P, PACK, CHUNK], F32, name="y", bufs=4)
             for pair in range(2):
-                acc = psum.tile([P, 2, CHUNK], F32, name="acc", tag="bank")
-                for u in range(2):
-                    t = 2 * pair + u
-                    for g in range(GROUPS):
-                        wcols = slice(g * N + t * P, g * N + (t + 1) * P)
-                        nc.tensor.matmul_mx(
-                            out=acc[:, u, :], lhsT=w4_c[:, wcols].bitcast(FP8X4), lhsT_scale=w4_s[:, wcols],
-                            rhs=z_c[g][:].bitcast(FP8X4), rhs_scale=z_s[g][:], start=(g == 0), stop=(g == GROUPS - 1),
-                        )
-                nc.scalar.copy(out=y[:, 2 * pair : 2 * pair + 2, :], in_=acc[:])
+                add_pass(acc[ch][pair], pair, 1, codes[:], scales[:])
+                nc.scalar.copy(out=y[:, 2 * pair : 2 * pair + 2, :], in_=acc[ch][pair][:])
             nc.sync.dma_start(out=y_rows[:, :, cols], in_=y[:])
-            y_b = work.tile([P, CHUNK * PACK], BF16, name="y_b", align_bytes=64)
-            nc.scalar.copy(
-                out=y_b[:].rearrange("p (c i t) -> p c t i", i=4, t=PACK),
-                in_=y[:].rearrange("p t (c i) -> p c t i", i=4),
-            )
+            y_b = work.tile([P, CHUNK * PACK], BF16, name="y_b", align_bytes=64, bufs=4)
+            interleave(nc.vector.tensor_copy if ch % 2 else nc.scalar.copy, y_b[:], y[:])
             return y_b
 
         def score_planes(ch, y_b):
@@ -243,6 +285,8 @@ def tile_list_deadlock_risk_scores_kernel(
 
         rounded = []
         for ch in range(M // CHUNK):
+            if ch % 2 == 0:
+                first_pass(ch // 2)
             rounded.append(scores(ch))
             if ch >= 1:
                 score_planes(ch - 1, rounded[ch - 1])

@@ -41,7 +41,7 @@ def tile_list_deadlock_risk_scores_kernel(
         fetch = keep.tile([P, M // STRIPE], U16, name="fetch")
 
         def load_rows(src, cols):
-            raw = work.tile([P, PACK, PASS], F32, name="raw", bufs=3)
+            raw = work.tile([P, PACK, PASS], F32, name="raw")
             nc.sync.dma_start(out=raw[:], in_=src.rearrange("(p j) c -> p j c", j=PACK)[:, :, cols])
             return raw
 
@@ -111,9 +111,10 @@ def tile_list_deadlock_risk_scores_kernel(
         nc.vector.memset(warm[:], 1.0)
         nc.scalar.activation(out=warm[:], in_=warm[:], func=ACT.Abs_reciprocal_sqrt)
 
-        pages = [keep.tile([P, T2], F32, name="page%d" % i) for i in range(2)]
-        for page in pages:
-            nc.vector.memset(page[:].bitcast(I32), 0)
+        page_first = keep.tile([P, T2], F32, name="page_first")
+        nc.vector.memset(page_first[:].bitcast(I32), 0)
+        page_third = keep.tile([P, T2], F32, name="page_third")
+        nc.gpsimd.memset(page_third[:].bitcast(I32), 0)
 
         w1_c = keep.tile([P, H], U32, name="w1_c", align_bytes=64)
         w1_s = keep.tile([P, H], U8, name="w1_s", align_bytes=64)
@@ -149,8 +150,14 @@ def tile_list_deadlock_risk_scores_kernel(
             v_s.append(scales)
 
         deal_words(1)
+        page_second = keep.tile([P, T2], F32, name="page_second", tag="tab_s")
+        nc.gpsimd.memset(page_second[:].bitcast(I32), 0)
+        pages = [page_first, page_second, page_third]
 
-        x = [keep.tile([P, PACK, M], BF16, name="x%d" % g) for g in range(GROUPS)]
+        slices = GROUPS * PACK
+        shared = [keep.tile([P, PACK * S], F32, name="shared%d" % g) for g in range(GROUPS)]
+        damp_first = keep.tile([P, S], F32, name="damp_first")
+        x = [tile[:].bitcast(BF16).rearrange("p (t w) -> p t w", t=PACK)[:, :, 0:M] for tile in shared]
         ceil = [keep.tile([P, M * PACK], BF16, name="ceil%d" % g, align_bytes=64) for g in range(GROUPS)]
         h = [keep.tile([P, S], F32, name="h%d" % i, align_bytes=64) for i in range(2)]
 
@@ -159,19 +166,25 @@ def tile_list_deadlock_risk_scores_kernel(
             rows = slice(s * P, (s + 1) * P)
             lin = work.tile([P, S], F32, name="lin", bufs=3)
             gate = work.tile([P, S], F32, name="gate") if s > 0 else None
-            damp = work.tile([P, S], F32, name="damp", bufs=3)
-            by_halves = s < 3
-            for half in range(S // BANK):
-                cols = slice(half * BANK, (half + 1) * BANK)
-                moving = dict(rhs=v_c[half][:].bitcast(FP8X4), rhs_scale=v_s[half][:], start=True, stop=True)
-                c = psum.tile([P, BANK], F32, name="c", tag="bank")
+            before = (s - 1) % PACK
+            damp = damp_first if s == 0 else shared[(s - 1) // PACK][:, before * S : (before + 1) * S]
+            widths = (256, 256, 512) if s == 0 else (BANK, BANK)
+            whole = s >= PACK
+            first = 0
+            for width in widths:
+                cols = slice(first, first + width)
+                half, inner = divmod(first, BANK)
+                inner = slice(inner, inner + width)
+                first = first + width
+                moving = dict(rhs=v_c[half][:, inner].bitcast(FP8X4), rhs_scale=v_s[half][:, inner], start=True, stop=True)
+                c = psum.tile([P, width], F32, name="c", tag="bank")
                 nc.tensor.matmul_mx(out=c[:], lhsT=w3_c[:, rows].bitcast(FP8X4), lhsT_scale=w23_s[4:P, rows], **moving)
-                b = psum.tile([P, BANK], F32, name="b", tag="bank")
+                a = psum.tile([P, width], F32, name="a", tag="bank")
+                nc.tensor.matmul_mx(out=a[:], lhsT=w1_c[:, rows].bitcast(FP8X4), lhsT_scale=w1_s[:, rows], **moving)
+                b = psum.tile([P, width], F32, name="b", tag="bank")
                 nc.tensor.matmul_mx(
                     out=b[:], lhsT=w2_c[:, 2 * s * P : 2 * (s + 1) * P].bitcast(FP4X4), lhsT_scale=w23_s[:, rows], **moving
                 )
-                a = psum.tile([P, BANK], F32, name="a", tag="bank")
-                nc.tensor.matmul_mx(out=a[:], lhsT=w1_c[:, rows].bitcast(FP8X4), lhsT_scale=w1_s[:, rows], **moving)
                 nc.scalar.activation(out=damp[:, cols], in_=c[:], func=ACT.Abs)
                 nc.scalar.copy(out=lin[:, cols], in_=a[:])
                 if s == 0:
@@ -180,27 +193,28 @@ def tile_list_deadlock_risk_scores_kernel(
                     )
                 else:
                     nc.scalar.activation(out=gate[:, cols], in_=b[:], func=ACT.Relu)
-                if by_halves or half == 1:
-                    cols = cols if by_halves else slice(0, S)
-                    nc.scalar.activation(out=damp[:, cols], in_=damp[:, cols], func=ACT.Abs_reciprocal_sqrt, bias=1.0)
-                    nc.scalar.activation(out=damp[:, cols], in_=damp[:, cols], func=ACT.Square)
-                    engine = nc.vector if s == 0 else nc.gpsimd
-                    if s > 0:
-                        engine.tensor_tensor(out=lin[:, cols], in0=lin[:, cols], in1=gate[:, cols], op=ALU.add)
-                    engine.tensor_tensor(out=damp[:, cols], in0=damp[:, cols], in1=wg[t][:, cols], op=ALU.mult)
-                    engine.tensor_tensor(out=h[s % 2][:, cols], in0=lin[:, cols], in1=damp[:, cols], op=ALU.mult)
-                    entries = put[:, cols.start // STRIPE : cols.stop // STRIPE]
-                    nc.vector.tensor_copy(out=pages[s % 2][:].indirect(entries), in_=h[s % 2][:, cols])
+                if whole:
+                    if first < S:
+                        continue
+                    cols = slice(0, S)
+                nc.scalar.activation(out=damp[:, cols], in_=damp[:, cols], func=ACT.Abs_reciprocal_sqrt, bias=1.0)
+                nc.scalar.activation(out=damp[:, cols], in_=damp[:, cols], func=ACT.Square)
+                engine = nc.vector if width < BANK else nc.gpsimd
+                if s > 0:
+                    engine.tensor_tensor(out=lin[:, cols], in0=lin[:, cols], in1=gate[:, cols], op=ALU.add)
+                engine.tensor_tensor(out=damp[:, cols], in0=damp[:, cols], in1=wg[t][:, cols], op=ALU.mult)
+                engine.tensor_tensor(out=h[s % 2][:, cols], in0=lin[:, cols], in1=damp[:, cols], op=ALU.mult)
+                entries = put[:, cols.start // STRIPE : cols.stop // STRIPE]
+                nc.vector.tensor_copy(out=pages[s % 3][:].indirect(entries), in_=h[s % 2][:, cols])
 
         def fetch_columns(s, cols):
             g, t = divmod(s, PACK)
             entries = fetch[:, cols.start // STRIPE : cols.stop // STRIPE]
-            nc.vector.tensor_copy(out=x[g][:, t, cols], in_=pages[s % 2][:].indirect(entries))
+            nc.vector.tensor_copy(out=x[g][:, t, cols], in_=pages[s % 3][:].indirect(entries))
 
         def words(ch, width=CHUNK):
             return slice(ch * width * PACK, (ch + 1) * width * PACK)
 
-        slices = GROUPS * PACK
         w4_grouped = []
         for s in range(slices):
             features(s)
@@ -225,6 +239,8 @@ def tile_list_deadlock_risk_scores_kernel(
         w4_s = keep.tile([P, GROUPS * N], U8, name="w4_s", align_bytes=64)
         for g in range(GROUPS):
             quantise(w4_grouped[g][:], w4_c[:, g * N : (g + 1) * N], w4_s[:, g * N : (g + 1) * N])
+        edges = (0, 256, 512, 768, 896, 1024)
+        chunks = [slice(lo, hi) for lo, hi in zip(edges[:-1], edges[1:])]
         for ch in range(M // CHUNK):
             fetch_columns(slices - 1, slice(ch * CHUNK, (ch + 1) * CHUNK))
         for ch in range(M // CHUNK):
@@ -245,53 +261,57 @@ def tile_list_deadlock_risk_scores_kernel(
             quantise(z, codes[:], scales[:])
             return codes, scales
 
-        def add_pass(acc, pair, g, codes, scales):
-            for u in range(2):
-                t = 2 * pair + u
+        def add_pass(banks, g, codes, scales):
+            per_bank = PACK // len(banks)
+            for t in range(PACK):
                 wcols = slice(g * N + t * P, g * N + (t + 1) * P)
+                bank, u = divmod(t, per_bank)
                 nc.tensor.matmul_mx(
-                    out=acc[:, u, :], lhsT=w4_c[:, wcols].bitcast(FP8X4), lhsT_scale=w4_s[:, wcols],
-                    rhs=codes.bitcast(FP8X4), rhs_scale=scales, start=(g == 0 and u == 0), stop=(g == 1 and u == 1),
+                    out=banks[bank][:, u, :], lhsT=w4_c[:, wcols].bitcast(FP8X4), lhsT_scale=w4_s[:, wcols],
+                    rhs=codes.bitcast(FP8X4), rhs_scale=scales,
+                    start=(g == 0 and u == 0), stop=(g == GROUPS - 1 and u == per_bank - 1),
                 )
 
-        acc = []
+        acc = {}
 
-        def first_pass(half):
-            cols = slice(half * 2 * CHUNK, (half + 1) * 2 * CHUNK)
-            codes, scales = capped(0, cols, h[1][:].bitcast(BF16), "z0%d" % half)
-            for u in range(2):
-                part = slice(u * CHUNK, (u + 1) * CHUNK)
-                banks = [psum.tile([P, 2, CHUNK], F32, name="acc", tag="bank") for pair in range(2)]
-                for pair in range(2):
-                    add_pass(banks[pair], pair, 0, codes[:, part], scales[:, part])
-                acc.append(banks)
+        def first_pass(lo):
+            codes, scales = capped(0, slice(lo, lo + BANK), h[1][:].bitcast(BF16), "z0_%d" % lo)
+            for cols in chunks:
+                if lo <= cols.start < lo + BANK:
+                    width = cols.stop - cols.start
+                    per_bank = BANK // width
+                    banks = [psum.tile([P, per_bank, width], F32, name="acc", tag="bank") for i in range(PACK // per_bank)]
+                    part = slice(cols.start - lo, cols.stop - lo)
+                    add_pass(banks, 0, codes[:, part], scales[:, part])
+                    acc[cols.start] = banks
 
-        def scores(ch):
-            cols = slice(ch * CHUNK, (ch + 1) * CHUNK)
-            codes, scales = capped(1, cols, x_i[1][:, words(ch)], "z1%d" % ch)
-            y = work.tile([P, PACK, CHUNK], F32, name="y", bufs=4)
-            for pair in range(2):
-                add_pass(acc[ch][pair], pair, 1, codes[:], scales[:])
-                nc.scalar.copy(out=y[:, 2 * pair : 2 * pair + 2, :], in_=acc[ch][pair][:])
+        def scores(cols, copy):
+            width = cols.stop - cols.start
+            codes, scales = capped(1, cols, x_i[1][:, PACK * cols.start : PACK * cols.stop], "z1_%d" % cols.start)
+            y = keep.tile([P, PACK, width], F32, name="y%d" % cols.start)
+            banks = acc[cols.start]
+            add_pass(banks, 1, codes[:], scales[:])
+            per_bank = PACK // len(banks)
+            for i, bank in enumerate(banks):
+                nc.scalar.copy(out=y[:, i * per_bank : (i + 1) * per_bank, :], in_=bank[:])
             nc.sync.dma_start(out=y_rows[:, :, cols], in_=y[:])
-            y_b = work.tile([P, CHUNK * PACK], BF16, name="y_b", align_bytes=64, bufs=4)
-            interleave(nc.vector.tensor_copy if ch % 2 else nc.scalar.copy, y_b[:], y[:])
+            y_b = keep.tile([P, width * PACK], BF16, name="y_b%d" % cols.start, align_bytes=64)
+            interleave(copy, y_b[:], y[:])
             return y_b
 
-        def score_planes(ch, y_b):
-            cols = slice(ch * CHUNK, (ch + 1) * CHUNK)
-            nc.vector.quantize_mx(out=y_c[:, cols].bitcast(FP8X4), scales=y_s[:, cols], in_=y_b[:])
+        def score_planes(cols, y_b):
+            quantise(y_b[:], y_c[:, cols], y_s[:, cols])
             nc.sync.dma_start(out=y_words[:, cols], in_=y_c[:, cols])
 
         rounded = []
-        for ch in range(M // CHUNK):
-            if ch % 2 == 0:
-                first_pass(ch // 2)
-            rounded.append(scores(ch))
-            if ch >= 1:
-                score_planes(ch - 1, rounded[ch - 1])
-        score_planes(M // CHUNK - 1, rounded[-1])
+        for i, cols in enumerate(chunks):
+            if cols.start % BANK == 0:
+                first_pass(cols.start)
+            rounded.append(scores(cols, nc.scalar.copy if i < 2 else nc.vector.tensor_copy))
+            if i >= 1:
+                score_planes(chunks[i - 1], rounded[i - 1])
+        score_planes(chunks[-1], rounded[-1])
         for q in range(4):
-            nc.sync.dma_start(
+            (nc.sync if q < 2 else nc.scalar).dma_start(
                 out=out_2[0, 4 * q : 4 * q + 4, :].bitcast(I32), in_=y_s[32 * q : 32 * q + 4, :].bitcast(I32)
             )

@@ -20,9 +20,19 @@ P = 128
 PACK = 4
 PASS = P * PACK
 GROUPS = H // PASS
+SLICES = GROUPS * PACK
 BANK = 512
-CHUNK = 256
 STRIPE = 16
+QUADRANTS = 4
+W3_ROW = 4
+LINE = 4
+
+FIRST_WIDTHS = (256, 256, 512)
+VECTOR_SUMS = 2
+BY_HALVES = 4
+PAGES = 3
+PIECE = 256
+EDGES = (0, 256, 512, 768, 896, 1024)
 
 
 def tile_list_deadlock_risk_scores_kernel(
@@ -40,6 +50,12 @@ def tile_list_deadlock_risk_scores_kernel(
         put = keep.tile([P, S // STRIPE], U16, name="put")
         fetch = keep.tile([P, M // STRIPE], U16, name="fetch")
 
+        def entries(list_tile, cols):
+            return list_tile[:, cols.start // STRIPE : cols.stop // STRIPE]
+
+        def packed(cols):
+            return slice(PACK * cols.start, PACK * cols.stop)
+
         def load_rows(src, cols):
             raw = work.tile([P, PACK, PASS], F32, name="raw")
             nc.sync.dma_start(out=raw[:], in_=src.rearrange("(p j) c -> p j c", j=PACK)[:, :, cols])
@@ -53,16 +69,19 @@ def tile_list_deadlock_risk_scores_kernel(
             )
             return grouped
 
-        def quantise(grouped, codes, scales):
-            nc.vector.quantize_mx(out=codes.bitcast(FP8X4), scales=scales, in_=grouped)
+        def quantise(values, codes, scales):
+            nc.vector.quantize_mx(out=codes.bitcast(FP8X4), scales=scales, in_=values)
 
         def interleave(copy, out, planes):
-            copy(out=out.rearrange("p (c i t) -> p c t i", i=4, t=PACK), in_=planes.rearrange("p t (c i) -> p c t i", i=4))
+            copy(
+                out=out.rearrange("p (c i t) -> p c t i", i=LINE, t=PACK),
+                in_=planes.rearrange("p t (c i) -> p c t i", i=LINE),
+            )
 
-        def load_scale_rows(plane, first, src, quadrants):
+        def load_scale_rows(plane, row, src, quadrants):
             for q in quadrants:
                 nc.sync.dma_start(
-                    out=plane[32 * q + first : 32 * q + first + 4, :].bitcast(I32),
+                    out=plane[32 * q + row : 32 * q + row + 4, :].bitcast(I32),
                     in_=src[0, 4 * q : 4 * q + 4, :].bitcast(I32),
                 )
 
@@ -77,35 +96,36 @@ def tile_list_deadlock_risk_scores_kernel(
         w2_raw = [keep.tile([P, 2 * PASS], U8, name="w2_raw%d" % g) for g in range(GROUPS)]
 
         def load_words(g):
-            cols = slice(g * PASS, (g + 1) * PASS)
-            nc.sync.dma_start(out=w3_raw[g][:], in_=w3_words[0].rearrange("p n t -> p (n t)").bitcast(I32)[:, cols])
-            cols = slice(g * PASS // 2, (g + 1) * PASS // 2)
-            nc.sync.dma_start(out=w2_raw[g][:].bitcast(I32), in_=w2_words[0].bitcast(I32)[:, cols])
+            w3_view = w3_words[0].rearrange("p n t -> p (n t)").bitcast(I32)
+            nc.sync.dma_start(out=w3_raw[g][:], in_=w3_view[:, g * PASS : (g + 1) * PASS])
+            w2_view = w2_words[0].bitcast(I32)
+            nc.sync.dma_start(out=w2_raw[g][:].bitcast(I32), in_=w2_view[:, g * PASS // 2 : (g + 1) * PASS // 2])
 
-        load_scale_rows(w23_s_raw, 4, w3_scales, range(4))
-        load_scale_rows(w23_s_raw, 0, w2_scales, range(2))
+        load_scale_rows(w23_s_raw, W3_ROW, w3_scales, range(QUADRANTS))
+        load_scale_rows(w23_s_raw, 0, w2_scales, range(QUADRANTS // 2))
         load_words(0)
-        load_scale_rows(w23_s_raw, 0, w2_scales, range(2, 4))
-        load_scale_rows(tab_s, 0, tab_scales, range(4))
+        load_scale_rows(w23_s_raw, 0, w2_scales, range(QUADRANTS // 2, QUADRANTS))
+        load_scale_rows(tab_s, 0, tab_scales, range(QUADRANTS))
         tab_w = keep.tile([P, T], I32, name="tab_w", align_bytes=64)
         nc.sync.dma_start(out=tab_w[:], in_=tab_words[0].rearrange("p n t -> p (n t)").bitcast(I32))
-
         load_words(1)
+
         wgs_rows = wgs.rearrange("(m t) j -> m t j", t=PACK)
+        row_bytes = 4 * S
         wg_tiles = [
-            (keep.tile([P, 1, S], F32, name="wg0"), 0, 1),
-            (keep.tile([P, 1, S], F32, name="wg1"), 1, 2),
-            (late.tile([P, 2, S], F32, name="wg23", align_bytes=64, offset=4 * S), 2, 4),
+            keep.tile([P, 1, S], F32, name="wg0"),
+            late.tile([P, 1, S], F32, name="wg1", align_bytes=64, offset=row_bytes),
+            keep.tile([P, 1, S], F32, name="wg2"),
+            late.tile([P, 1, S], F32, name="wg3", align_bytes=64, offset=2 * row_bytes),
         ]
-        wg = []
-        for tile, first, last in wg_tiles:
-            for q in range(4):
-                nc.sync.dma_start(out=tile[32 * q : 32 * q + 32], in_=wgs_rows[:, first:last, :])
-            wg.extend(tile[:, t, :] for t in range(last - first))
-            if first == 0:
+        for t in range(PACK):
+            for q in range(QUADRANTS):
+                nc.sync.dma_start(out=wg_tiles[t][32 * q : 32 * q + 32], in_=wgs_rows[:, t : t + 1, :])
+            if t == 0:
                 nc.sync.dma_start(out=put[:], in_=offs2)
                 w1_raw.append(load_rows(w1, slice(PASS, H)))
                 nc.sync.dma_start(out=fetch[:], in_=offs3)
+        wg = [wg_tile[:, 0, :] for wg_tile in wg_tiles]
 
         warm = keep.tile([P, 8], F32, name="warm")
         nc.vector.memset(warm[:], 1.0)
@@ -141,44 +161,41 @@ def tile_list_deadlock_risk_scores_kernel(
 
         v_c, v_s = [], []
         for half in range(S // BANK):
-            entries = pick[:, half * BANK // STRIPE : (half + 1) * BANK // STRIPE]
-            scales = keep.tile([P, BANK], U8, name="v_s%d" % half, align_bytes=64)
-            nc.vector.tensor_copy(out=scales[:], in_=tab_s[:].indirect(entries))
-            codes = keep.tile([P, BANK], U32, name="v_c%d" % half, align_bytes=64)
-            nc.vector.tensor_copy(out=codes[:], in_=tab_w[:].bitcast(U32).indirect(entries))
-            v_c.append(codes)
-            v_s.append(scales)
+            picked = entries(pick, slice(half * BANK, (half + 1) * BANK))
+            v_s.append(keep.tile([P, BANK], U8, name="v_s%d" % half, align_bytes=64))
+            nc.vector.tensor_copy(out=v_s[half][:], in_=tab_s[:].indirect(picked))
+            v_c.append(keep.tile([P, BANK], U32, name="v_c%d" % half, align_bytes=64))
+            nc.vector.tensor_copy(out=v_c[half][:], in_=tab_w[:].bitcast(U32).indirect(picked))
 
         deal_words(1)
         page_second = keep.tile([P, T2], F32, name="page_second", tag="tab_s")
         nc.gpsimd.memset(page_second[:].bitcast(I32), 0)
         pages = [page_first, page_second, page_third]
+        assert len(pages) == PAGES
 
-        slices = GROUPS * PACK
         shared = [keep.tile([P, PACK * S], F32, name="shared%d" % g) for g in range(GROUPS)]
         damp_first = keep.tile([P, S], F32, name="damp_first")
-        x = [tile[:].bitcast(BF16).rearrange("p (t w) -> p t w", t=PACK)[:, :, 0:M] for tile in shared]
+        x = [both[:].bitcast(BF16).rearrange("p (t w) -> p t w", t=PACK)[:, :, 0:M] for both in shared]
         ceil = [keep.tile([P, M * PACK], BF16, name="ceil%d" % g, align_bytes=64) for g in range(GROUPS)]
         h = [keep.tile([P, S], F32, name="h%d" % i, align_bytes=64) for i in range(2)]
 
         def features(s):
-            g, t = divmod(s, PACK)
             rows = slice(s * P, (s + 1) * P)
             lin = work.tile([P, S], F32, name="lin", bufs=3)
-            gate = work.tile([P, S], F32, name="gate") if s > 0 else None
-            before = (s - 1) % PACK
-            damp = damp_first if s == 0 else shared[(s - 1) // PACK][:, before * S : (before + 1) * S]
-            widths = (256, 256, 512) if s == 0 else (BANK, BANK)
-            whole = s >= PACK
-            first = 0
-            for width in widths:
-                cols = slice(first, first + width)
-                half, inner = divmod(first, BANK)
-                inner = slice(inner, inner + width)
-                first = first + width
-                moving = dict(rhs=v_c[half][:, inner].bitcast(FP8X4), rhs_scale=v_s[half][:, inner], start=True, stop=True)
+            gate = work.tile([P, S], F32, name="gate") if s >= VECTOR_SUMS else None
+            g_before, t_before = divmod(s - 1, PACK)
+            damp = damp_first if s == 0 else shared[g_before][:, t_before * S : (t_before + 1) * S]
+            done = 0
+            for width in FIRST_WIDTHS if s == 0 else (BANK, BANK):
+                cols = slice(done, done + width)
+                half, inside = divmod(done, BANK)
+                part = slice(inside, inside + width)
+                done = done + width
+                moving = dict(rhs=v_c[half][:, part].bitcast(FP8X4), rhs_scale=v_s[half][:, part], start=True, stop=True)
                 c = psum.tile([P, width], F32, name="c", tag="bank")
-                nc.tensor.matmul_mx(out=c[:], lhsT=w3_c[:, rows].bitcast(FP8X4), lhsT_scale=w23_s[4:P, rows], **moving)
+                nc.tensor.matmul_mx(
+                    out=c[:], lhsT=w3_c[:, rows].bitcast(FP8X4), lhsT_scale=w23_s[W3_ROW:P, rows], **moving
+                )
                 a = psum.tile([P, width], F32, name="a", tag="bank")
                 nc.tensor.matmul_mx(out=a[:], lhsT=w1_c[:, rows].bitcast(FP8X4), lhsT_scale=w1_s[:, rows], **moving)
                 b = psum.tile([P, width], F32, name="b", tag="bank")
@@ -187,116 +204,118 @@ def tile_list_deadlock_risk_scores_kernel(
                 )
                 nc.scalar.activation(out=damp[:, cols], in_=c[:], func=ACT.Abs)
                 nc.scalar.copy(out=lin[:, cols], in_=a[:])
-                if s == 0:
+                if s < VECTOR_SUMS:
                     nc.vector.scalar_tensor_tensor(
                         out=lin[:, cols], in0=b[:], scalar=0.0, in1=lin[:, cols], op0=ALU.max, op1=ALU.add
                     )
                 else:
                     nc.scalar.activation(out=gate[:, cols], in_=b[:], func=ACT.Relu)
-                if whole:
-                    if first < S:
+                if s >= BY_HALVES:
+                    if done < S:
                         continue
                     cols = slice(0, S)
                 nc.scalar.activation(out=damp[:, cols], in_=damp[:, cols], func=ACT.Abs_reciprocal_sqrt, bias=1.0)
                 nc.scalar.activation(out=damp[:, cols], in_=damp[:, cols], func=ACT.Square)
                 engine = nc.vector if width < BANK else nc.gpsimd
-                if s > 0:
+                if s >= VECTOR_SUMS:
                     engine.tensor_tensor(out=lin[:, cols], in0=lin[:, cols], in1=gate[:, cols], op=ALU.add)
-                engine.tensor_tensor(out=damp[:, cols], in0=damp[:, cols], in1=wg[t][:, cols], op=ALU.mult)
+                engine.tensor_tensor(out=damp[:, cols], in0=damp[:, cols], in1=wg[s % PACK][:, cols], op=ALU.mult)
                 engine.tensor_tensor(out=h[s % 2][:, cols], in0=lin[:, cols], in1=damp[:, cols], op=ALU.mult)
-                entries = put[:, cols.start // STRIPE : cols.stop // STRIPE]
-                nc.vector.tensor_copy(out=pages[s % 3][:].indirect(entries), in_=h[s % 2][:, cols])
+                nc.vector.tensor_copy(out=pages[s % PAGES][:].indirect(entries(put, cols)), in_=h[s % 2][:, cols])
 
         def fetch_columns(s, cols):
             g, t = divmod(s, PACK)
-            entries = fetch[:, cols.start // STRIPE : cols.stop // STRIPE]
-            nc.vector.tensor_copy(out=x[g][:, t, cols], in_=pages[s % 3][:].indirect(entries))
+            nc.vector.tensor_copy(out=x[g][:, t, cols], in_=pages[s % PAGES][:].indirect(entries(fetch, cols)))
 
-        def words(ch, width=CHUNK):
-            return slice(ch * width * PACK, (ch + 1) * width * PACK)
+        pieces = [slice(lo, lo + PIECE) for lo in range(0, M, PIECE)]
+
+        def round_ceiling(g):
+            for lo in range(0, M, PASS):
+                raw = load_rows(ceiling[g * PASS : (g + 1) * PASS, :], slice(lo, lo + PASS))
+                for inside in range(0, PASS, PIECE):
+                    cols = slice(lo + inside, lo + inside + PIECE)
+                    interleave(nc.scalar.copy, ceil[g][:, packed(cols)], raw[:, :, inside : inside + PIECE])
 
         w4_grouped = []
-        for s in range(slices):
+        for s in range(SLICES):
             features(s)
             if s >= 1:
                 fetch_columns(s - 1, slice(0, M))
             if s == 0:
                 quantise(deal_columns(w1_raw[1])[:], w1_c[:, PASS:H], w1_s[:, PASS:H])
-        for g in range(GROUPS):
-            w4_grouped.append(deal_columns(load_rows(w4[g * PASS : (g + 1) * PASS, :], slice(0, N))))
-        for g in range(GROUPS):
-            for half in range(M // PASS):
-                raw = load_rows(ceiling[g * PASS : (g + 1) * PASS, :], slice(half * PASS, (half + 1) * PASS))
-                for u in range(PASS // CHUNK):
-                    interleave(nc.scalar.copy, ceil[g][:, words(2 * half + u)], raw[:, :, u * CHUNK : (u + 1) * CHUNK])
+            item = s - 2
+            if 0 <= item < GROUPS:
+                w4_grouped.append(deal_columns(load_rows(w4[item * PASS : (item + 1) * PASS, :], slice(0, N))))
+            if item == GROUPS:
+                round_ceiling(0)
+
         x_i = [
             late.tile([P, M * PACK], BF16, name="x_i0", align_bytes=64, offset=0),
             keep.tile([P, M * PACK], BF16, name="x_i1", tag="tab_w", align_bytes=64),
         ]
-        for ch in range(M // CHUNK):
-            interleave(nc.scalar.copy, x_i[0][:, words(ch)], x[0][:, :, ch * CHUNK : (ch + 1) * CHUNK])
-        w4_c = late.tile([P, GROUPS * N], U32, name="w4_c", align_bytes=64, offset=2 * M * PACK)
+        for cols in pieces:
+            interleave(nc.scalar.copy, x_i[0][:, packed(cols)], x[0][:, :, cols])
+        round_ceiling(1)
+        w4_c = late.tile([P, GROUPS * N], U32, name="w4_c", align_bytes=64, offset=2 * row_bytes)
         w4_s = keep.tile([P, GROUPS * N], U8, name="w4_s", align_bytes=64)
         for g in range(GROUPS):
             quantise(w4_grouped[g][:], w4_c[:, g * N : (g + 1) * N], w4_s[:, g * N : (g + 1) * N])
-        edges = (0, 256, 512, 768, 896, 1024)
-        chunks = [slice(lo, hi) for lo, hi in zip(edges[:-1], edges[1:])]
-        for ch in range(M // CHUNK):
-            fetch_columns(slices - 1, slice(ch * CHUNK, (ch + 1) * CHUNK))
-        for ch in range(M // CHUNK):
-            interleave(nc.scalar.copy, x_i[1][:, words(ch)], x[1][:, :, ch * CHUNK : (ch + 1) * CHUNK])
+        for cols in pieces:
+            fetch_columns(SLICES - 1, cols)
+        for cols in pieces:
+            interleave(nc.scalar.copy, x_i[1][:, packed(cols)], x[1][:, :, cols])
 
+        chunks = [slice(lo, hi) for lo, hi in zip(EDGES[:-1], EDGES[1:])]
         y_c = keep.tile([P, M], I32, name="y_c", align_bytes=64)
         y_s = keep.tile([P, M], U8, name="y_s", align_bytes=64)
         y_rows = out_0.rearrange("(p t) m -> p t m", t=PACK)
         y_words = out_1[0].rearrange("p m t -> p (m t)").bitcast(I32)
 
-        def capped(g, cols, z, name):
-            nc.vector.tensor_tensor(
-                out=z, in0=x_i[g][:, PACK * cols.start : PACK * cols.stop],
-                in1=ceil[g][:, PACK * cols.start : PACK * cols.stop], op=ALU.min,
-            )
-            codes = keep.tile([P, cols.stop - cols.start], U32, name=name + "_c", align_bytes=64)
-            scales = keep.tile([P, cols.stop - cols.start], U8, name=name + "_s", align_bytes=64)
-            quantise(z, codes[:], scales[:])
-            return codes, scales
+        def capped(g, cols):
+            z = x_i[g][:, packed(cols)]
+            nc.vector.tensor_tensor(out=z, in0=z, in1=ceil[g][:, packed(cols)], op=ALU.min)
+            width = cols.stop - cols.start
+            z_c = keep.tile([P, width], U32, name="z%d_%d_c" % (g, cols.start), align_bytes=64)
+            z_s = keep.tile([P, width], U8, name="z%d_%d_s" % (g, cols.start), align_bytes=64)
+            quantise(z, z_c[:], z_s[:])
+            return z_c, z_s
 
-        def add_pass(banks, g, codes, scales):
+        def add_pass(banks, g, z_c, z_s):
             per_bank = PACK // len(banks)
             for t in range(PACK):
                 wcols = slice(g * N + t * P, g * N + (t + 1) * P)
-                bank, u = divmod(t, per_bank)
+                bank, place = divmod(t, per_bank)
                 nc.tensor.matmul_mx(
-                    out=banks[bank][:, u, :], lhsT=w4_c[:, wcols].bitcast(FP8X4), lhsT_scale=w4_s[:, wcols],
-                    rhs=codes.bitcast(FP8X4), rhs_scale=scales,
-                    start=(g == 0 and u == 0), stop=(g == GROUPS - 1 and u == per_bank - 1),
+                    out=banks[bank][:, place, :], lhsT=w4_c[:, wcols].bitcast(FP8X4), lhsT_scale=w4_s[:, wcols],
+                    rhs=z_c.bitcast(FP8X4), rhs_scale=z_s,
+                    start=(g == 0 and place == 0), stop=(g == GROUPS - 1 and place == per_bank - 1),
                 )
 
-        acc = {}
-
-        def first_pass(lo):
-            codes, scales = capped(0, slice(lo, lo + BANK), h[1][:].bitcast(BF16), "z0_%d" % lo)
+        sums = {}
+        for lo in range(0, M, BANK):
+            z_c, z_s = capped(0, slice(lo, lo + BANK))
             for cols in chunks:
                 if lo <= cols.start < lo + BANK:
                     width = cols.stop - cols.start
                     per_bank = BANK // width
-                    banks = [psum.tile([P, per_bank, width], F32, name="acc", tag="bank") for i in range(PACK // per_bank)]
+                    sums[cols.start] = [
+                        psum.tile([P, per_bank, width], F32, name="acc", tag="bank") for i in range(PACK // per_bank)
+                    ]
                     part = slice(cols.start - lo, cols.stop - lo)
-                    add_pass(banks, 0, codes[:, part], scales[:, part])
-                    acc[cols.start] = banks
+                    add_pass(sums[cols.start], 0, z_c[:, part], z_s[:, part])
 
-        def scores(cols, copy):
+        def scores(cols):
             width = cols.stop - cols.start
-            codes, scales = capped(1, cols, x_i[1][:, PACK * cols.start : PACK * cols.stop], "z1_%d" % cols.start)
+            z_c, z_s = capped(1, cols)
             y = keep.tile([P, PACK, width], F32, name="y%d" % cols.start)
-            banks = acc[cols.start]
-            add_pass(banks, 1, codes[:], scales[:])
+            banks = sums[cols.start]
+            add_pass(banks, 1, z_c[:], z_s[:])
             per_bank = PACK // len(banks)
             for i, bank in enumerate(banks):
                 nc.scalar.copy(out=y[:, i * per_bank : (i + 1) * per_bank, :], in_=bank[:])
             nc.sync.dma_start(out=y_rows[:, :, cols], in_=y[:])
             y_b = keep.tile([P, width * PACK], BF16, name="y_b%d" % cols.start, align_bytes=64)
-            interleave(copy, y_b[:], y[:])
+            interleave(nc.vector.tensor_copy, y_b[:], y[:])
             return y_b
 
         def score_planes(cols, y_b):
@@ -305,13 +324,11 @@ def tile_list_deadlock_risk_scores_kernel(
 
         rounded = []
         for i, cols in enumerate(chunks):
-            if cols.start % BANK == 0:
-                first_pass(cols.start)
-            rounded.append(scores(cols, nc.scalar.copy if i < 2 else nc.vector.tensor_copy))
+            rounded.append(scores(cols))
             if i >= 1:
                 score_planes(chunks[i - 1], rounded[i - 1])
         score_planes(chunks[-1], rounded[-1])
-        for q in range(4):
-            (nc.sync if q < 2 else nc.scalar).dma_start(
+        for q in range(QUADRANTS):
+            (nc.sync if q < QUADRANTS // 2 else nc.scalar).dma_start(
                 out=out_2[0, 4 * q : 4 * q + 4, :].bitcast(I32), in_=y_s[32 * q : 32 * q + 4, :].bitcast(I32)
             )

from contextlib import ExitStack

import concourse.mybir as mybir

K, H, N, T, S, T2, M = 512, 1024, 512, 4096, 1024, 2048, 1024
FLOPS = 2 * K * H * S * 3 + 2 * H * N * M

F32 = mybir.dt.float32
BF16 = mybir.dt.bfloat16
I32 = mybir.dt.int32
U32 = mybir.dt.uint32
U16 = mybir.dt.uint16
U8 = mybir.dt.uint8
FP8X4 = mybir.dt.float8_e4m3fn_x4
FP4X4 = mybir.dt.float4_e2m1fn_x4
ACT = mybir.ActivationFunctionType
ALU = mybir.AluOpType

P = 128
PACK = 4
PASS = P * PACK
GROUPS = H // PASS
SLICES = GROUPS * PACK
BANK = 512
STRIPE = 16
QUADRANTS = 4
W3_ROW = 4
LINE = 4

FIRST_WIDTHS = (256, 256, 512)
VECTOR_SUMS = 2
BY_HALVES = 4
PAGES = 3
PIECE = 256
EDGES = (0, 256, 512, 768, 896, 1024)


def tile_list_deadlock_risk_scores_kernel(
    tc, tab_words, tab_scales, offs, w1, w2_words, w2_scales, w3_words, w3_scales,
    offs2, wgs, offs3, ceiling, w4, out_0, out_1, out_2,
):
    nc = tc.nc
    with ExitStack() as ctx:
        keep = ctx.enter_context(tc.tile_pool(name="keep", bufs=1))
        work = ctx.enter_context(tc.tile_pool(name="work", bufs=2))
        late = ctx.enter_context(tc.tile_pool(name="late", bufs=1))
        psum = ctx.enter_context(tc.psum_pool(name="psum", bufs=8))

        pick = keep.tile([P, S // STRIPE], U16, name="pick")
        put = keep.tile([P, S // STRIPE], U16, name="put")
        fetch = keep.tile([P, M // STRIPE], U16, name="fetch")

        def entries(list_tile, cols):
            return list_tile[:, cols.start // STRIPE : cols.stop // STRIPE]

        def packed(cols):
            return slice(PACK * cols.start, PACK * cols.stop)

        def load_rows(src, cols):
            raw = work.tile([P, PACK, PASS], F32, name="raw")
            nc.sync.dma_start(out=raw[:], in_=src.rearrange("(p j) c -> p j c", j=PACK)[:, :, cols])
            return raw

        def deal_columns(raw):
            grouped = work.tile([P, PASS * PACK], BF16, name="grouped", align_bytes=64)
            nc.scalar.copy(
                out=grouped[:].rearrange("p (t m j) -> p m j t", t=PACK, j=PACK),
                in_=raw[:].rearrange("p j (m t) -> p m j t", t=PACK),
            )
            return grouped

        def quantise(values, codes, scales):
            nc.vector.quantize_mx(out=codes.bitcast(FP8X4), scales=scales, in_=values)

        def interleave(copy, out, planes):
            copy(
                out=out.rearrange("p (c i t) -> p c t i", i=LINE, t=PACK),
                in_=planes.rearrange("p t (c i) -> p c t i", i=LINE),
            )

        def load_scale_rows(plane, row, src, quadrants):
            for q in quadrants:
                nc.sync.dma_start(
                    out=plane[32 * q + row : 32 * q + row + 4, :].bitcast(I32),
                    in_=src[0, 4 * q : 4 * q + 4, :].bitcast(I32),
                )

        tab_s = keep.tile([P, T], U8, name="tab_s")
        nc.vector.memset(tab_s[:].bitcast(I32), 0)
        w23_s_raw = keep.tile([P, H], U8, name="w23_s_raw")
        nc.gpsimd.memset(w23_s_raw[:].bitcast(I32), 0)

        nc.sync.dma_start(out=pick[:], in_=offs)
        w1_raw = [load_rows(w1, slice(0, PASS))]
        w3_raw = [keep.tile([P, PASS], I32, name="w3_raw%d" % g) for g in range(GROUPS)]
        w2_raw = [keep.tile([P, 2 * PASS], U8, name="w2_raw%d" % g) for g in range(GROUPS)]

        def load_words(g):
            w3_view = w3_words[0].rearrange("p n t -> p (n t)").bitcast(I32)
            nc.sync.dma_start(out=w3_raw[g][:], in_=w3_view[:, g * PASS : (g + 1) * PASS])
            w2_view = w2_words[0].bitcast(I32)
            nc.sync.dma_start(out=w2_raw[g][:].bitcast(I32), in_=w2_view[:, g * PASS // 2 : (g + 1) * PASS // 2])

        load_scale_rows(w23_s_raw, W3_ROW, w3_scales, range(QUADRANTS))
        load_scale_rows(w23_s_raw, 0, w2_scales, range(QUADRANTS // 2))
        load_words(0)
        load_scale_rows(w23_s_raw, 0, w2_scales, range(QUADRANTS // 2, QUADRANTS))
        load_scale_rows(tab_s, 0, tab_scales, range(QUADRANTS))
        tab_w = keep.tile([P, T], I32, name="tab_w", align_bytes=64)
        nc.sync.dma_start(out=tab_w[:], in_=tab_words[0].rearrange("p n t -> p (n t)").bitcast(I32))
        load_words(1)

        wgs_rows = wgs.rearrange("(m t) j -> m t j", t=PACK)
        row_bytes = 4 * S
        wg_tiles = [
            keep.tile([P, 1, S], F32, name="wg0"),
            late.tile([P, 1, S], F32, name="wg1", align_bytes=64, offset=row_bytes),
            keep.tile([P, 1, S], F32, name="wg2"),
            late.tile([P, 1, S], F32, name="wg3", align_bytes=64, offset=2 * row_bytes),
        ]
        for t in range(PACK):
            for q in range(QUADRANTS):
                nc.sync.dma_start(out=wg_tiles[t][32 * q : 32 * q + 32], in_=wgs_rows[:, t : t + 1, :])
            if t == 0:
                nc.sync.dma_start(out=put[:], in_=offs2)
                w1_raw.append(load_rows(w1, slice(PASS, H)))
                nc.sync.dma_start(out=fetch[:], in_=offs3)
        wg = [wg_tile[:, 0, :] for wg_tile in wg_tiles]

        warm = keep.tile([P, 8], F32, name="warm")
        nc.vector.memset(warm[:], 1.0)
        nc.scalar.activation(out=warm[:], in_=warm[:], func=ACT.Abs_reciprocal_sqrt)

        page_first = keep.tile([P, T2], F32, name="page_first")
        nc.vector.memset(page_first[:].bitcast(I32), 0)
        page_third = keep.tile([P, T2], F32, name="page_third")
        nc.gpsimd.memset(page_third[:].bitcast(I32), 0)

        w1_c = keep.tile([P, H], U32, name="w1_c", align_bytes=64)
        w1_s = keep.tile([P, H], U8, name="w1_s", align_bytes=64)
        quantise(deal_columns(w1_raw[0])[:], w1_c[:, 0:PASS], w1_s[:, 0:PASS])
        w3_c = keep.tile([P, H], I32, name="w3_c", align_bytes=64)
        w2_c = keep.tile([P, 2 * H], U8, name="w2_c", align_bytes=64)

        def deal_words(g):
            nc.vector.tensor_copy(
                out=w3_c[:, g * PASS : (g + 1) * PASS].rearrange("p (t m) -> p m t", t=PACK),
                in_=w3_raw[g][:].rearrange("p (m t) -> p m t", t=PACK),
            )
            nc.vector.tensor_copy(
                out=w2_c[:, 2 * g * PASS : 2 * (g + 1) * PASS].rearrange("p (t m b) -> p m t b", t=PACK, b=2),
                in_=w2_raw[g][:].rearrange("p (m t b) -> p m t b", t=PACK, b=2),
            )

        deal_words(0)
        w23_s = keep.tile([P, H], U8, name="w23_s", align_bytes=64)
        nc.vector.tensor_copy(
            out=w23_s[:].rearrange("p (g t m) -> p g m t", g=GROUPS, t=PACK),
            in_=w23_s_raw[:].rearrange("p (g m t) -> p g m t", g=GROUPS, t=PACK),
        )

        v_c, v_s = [], []
        for half in range(S // BANK):
            picked = entries(pick, slice(half * BANK, (half + 1) * BANK))
            v_s.append(keep.tile([P, BANK], U8, name="v_s%d" % half, align_bytes=64))
            nc.vector.tensor_copy(out=v_s[half][:], in_=tab_s[:].indirect(picked))
            v_c.append(keep.tile([P, BANK], U32, name="v_c%d" % half, align_bytes=64))
            nc.vector.tensor_copy(out=v_c[half][:], in_=tab_w[:].bitcast(U32).indirect(picked))

        deal_words(1)
        page_second = keep.tile([P, T2], F32, name="page_second", tag="tab_s")
        nc.gpsimd.memset(page_second[:].bitcast(I32), 0)
        pages = [page_first, page_second, page_third]
        assert len(pages) == PAGES

        shared = [keep.tile([P, PACK * S], F32, name="shared%d" % g) for g in range(GROUPS)]
        damp_first = keep.tile([P, S], F32, name="damp_first")
        x = [both[:].bitcast(BF16).rearrange("p (t w) -> p t w", t=PACK)[:, :, 0:M] for both in shared]
        ceil = [keep.tile([P, M * PACK], BF16, name="ceil%d" % g, align_bytes=64) for g in range(GROUPS)]
        h = [keep.tile([P, S], F32, name="h%d" % i, align_bytes=64) for i in range(2)]

        def features(s):
            rows = slice(s * P, (s + 1) * P)
            lin = work.tile([P, S], F32, name="lin", bufs=3)
            gate = work.tile([P, S], F32, name="gate") if s >= VECTOR_SUMS else None
            g_before, t_before = divmod(s - 1, PACK)
            damp = damp_first if s == 0 else shared[g_before][:, t_before * S : (t_before + 1) * S]
            done = 0
            for width in FIRST_WIDTHS if s == 0 else (BANK, BANK):
                cols = slice(done, done + width)
                half, inside = divmod(done, BANK)
                part = slice(inside, inside + width)
                done = done + width
                moving = dict(rhs=v_c[half][:, part].bitcast(FP8X4), rhs_scale=v_s[half][:, part], start=True, stop=True)
                c = psum.tile([P, width], F32, name="c", tag="bank")
                nc.tensor.matmul_mx(
                    out=c[:], lhsT=w3_c[:, rows].bitcast(FP8X4), lhsT_scale=w23_s[W3_ROW:P, rows], **moving
                )
                a = psum.tile([P, width], F32, name="a", tag="bank")
                nc.tensor.matmul_mx(out=a[:], lhsT=w1_c[:, rows].bitcast(FP8X4), lhsT_scale=w1_s[:, rows], **moving)
                b = psum.tile([P, width], F32, name="b", tag="bank")
                nc.tensor.matmul_mx(
                    out=b[:], lhsT=w2_c[:, 2 * s * P : 2 * (s + 1) * P].bitcast(FP4X4), lhsT_scale=w23_s[:, rows], **moving
                )
                nc.scalar.activation(out=damp[:, cols], in_=c[:], func=ACT.Abs)
                nc.scalar.copy(out=lin[:, cols], in_=a[:])
                if s < VECTOR_SUMS:
                    nc.vector.scalar_tensor_tensor(
                        out=lin[:, cols], in0=b[:], scalar=0.0, in1=lin[:, cols], op0=ALU.max, op1=ALU.add
                    )
                else:
                    nc.scalar.activation(out=gate[:, cols], in_=b[:], func=ACT.Relu)
                if s >= BY_HALVES:
                    if done < S:
                        continue
                    cols = slice(0, S)
                nc.scalar.activation(out=damp[:, cols], in_=damp[:, cols], func=ACT.Abs_reciprocal_sqrt, bias=1.0)
                nc.scalar.activation(out=damp[:, cols], in_=damp[:, cols], func=ACT.Square)
                engine = nc.vector if width < BANK else nc.gpsimd
                if s >= VECTOR_SUMS:
                    engine.tensor_tensor(out=lin[:, cols], in0=lin[:, cols], in1=gate[:, cols], op=ALU.add)
                engine.tensor_tensor(out=damp[:, cols], in0=damp[:, cols], in1=wg[s % PACK][:, cols], op=ALU.mult)
                engine.tensor_tensor(out=h[s % 2][:, cols], in0=lin[:, cols], in1=damp[:, cols], op=ALU.mult)
                nc.vector.tensor_copy(out=pages[s % PAGES][:].indirect(entries(put, cols)), in_=h[s % 2][:, cols])

        def fetch_columns(s, cols):
            g, t = divmod(s, PACK)
            nc.vector.tensor_copy(out=x[g][:, t, cols], in_=pages[s % PAGES][:].indirect(entries(fetch, cols)))

        pieces = [slice(lo, lo + PIECE) for lo in range(0, M, PIECE)]

        def round_ceiling(g):
            for lo in range(0, M, PASS):
                raw = load_rows(ceiling[g * PASS : (g + 1) * PASS, :], slice(lo, lo + PASS))
                for inside in range(0, PASS, PIECE):
                    cols = slice(lo + inside, lo + inside + PIECE)
                    interleave(nc.scalar.copy, ceil[g][:, packed(cols)], raw[:, :, inside : inside + PIECE])

        w4_grouped = []
        for s in range(SLICES):
            features(s)
            if s >= 1:
                fetch_columns(s - 1, slice(0, M))
            if s == 0:
                quantise(deal_columns(w1_raw[1])[:], w1_c[:, PASS:H], w1_s[:, PASS:H])
            item = s - 2
            if 0 <= item < GROUPS:
                w4_grouped.append(deal_columns(load_rows(w4[item * PASS : (item + 1) * PASS, :], slice(0, N))))
            if item == GROUPS:
                round_ceiling(0)

        x_i = [
            late.tile([P, M * PACK], BF16, name="x_i0", align_bytes=64, offset=0),
            keep.tile([P, M * PACK], BF16, name="x_i1", tag="tab_w", align_bytes=64),
        ]
        for cols in pieces:
            interleave(nc.scalar.copy, x_i[0][:, packed(cols)], x[0][:, :, cols])
        round_ceiling(1)
        w4_c = late.tile([P, GROUPS * N], U32, name="w4_c", align_bytes=64, offset=2 * row_bytes)
        w4_s = keep.tile([P, GROUPS * N], U8, name="w4_s", align_bytes=64)
        for g in range(GROUPS):
            quantise(w4_grouped[g][:], w4_c[:, g * N : (g + 1) * N], w4_s[:, g * N : (g + 1) * N])
        for cols in pieces:
            fetch_columns(SLICES - 1, cols)
        for cols in pieces:
            interleave(nc.scalar.copy, x_i[1][:, packed(cols)], x[1][:, :, cols])

        chunks = [slice(lo, hi) for lo, hi in zip(EDGES[:-1], EDGES[1:])]
        y_c = keep.tile([P, M], I32, name="y_c", align_bytes=64)
        y_s = keep.tile([P, M], U8, name="y_s", align_bytes=64)
        y_rows = out_0.rearrange("(p t) m -> p t m", t=PACK)
        y_words = out_1[0].rearrange("p m t -> p (m t)").bitcast(I32)

        def capped(g, cols):
            z = x_i[g][:, packed(cols)]
            nc.vector.tensor_tensor(out=z, in0=z, in1=ceil[g][:, packed(cols)], op=ALU.min)
            width = cols.stop - cols.start
            z_c = keep.tile([P, width], U32, name="z%d_%d_c" % (g, cols.start), align_bytes=64)
            z_s = keep.tile([P, width], U8, name="z%d_%d_s" % (g, cols.start), align_bytes=64)
            quantise(z, z_c[:], z_s[:])
            return z_c, z_s

        def add_pass(banks, g, z_c, z_s):
            per_bank = PACK // len(banks)
            for t in range(PACK):
                wcols = slice(g * N + t * P, g * N + (t + 1) * P)
                bank, place = divmod(t, per_bank)
                nc.tensor.matmul_mx(
                    out=banks[bank][:, place, :], lhsT=w4_c[:, wcols].bitcast(FP8X4), lhsT_scale=w4_s[:, wcols],
                    rhs=z_c.bitcast(FP8X4), rhs_scale=z_s,
                    start=(g == 0 and place == 0), stop=(g == GROUPS - 1 and place == per_bank - 1),
                )

        sums = {}
        for lo in range(0, M, BANK):
            z_c, z_s = capped(0, slice(lo, lo + BANK))
            for cols in chunks:
                if lo <= cols.start < lo + BANK:
                    width = cols.stop - cols.start
                    per_bank = BANK // width
                    sums[cols.start] = [
                        psum.tile([P, per_bank, width], F32, name="acc", tag="bank") for i in range(PACK // per_bank)
                    ]
                    part = slice(cols.start - lo, cols.stop - lo)
                    add_pass(sums[cols.start], 0, z_c[:, part], z_s[:, part])

        def scores(cols):
            width = cols.stop - cols.start
            z_c, z_s = capped(1, cols)
            y = keep.tile([P, PACK, width], F32, name="y%d" % cols.start)
            banks = sums[cols.start]
            add_pass(banks, 1, z_c[:], z_s[:])
            per_bank = PACK // len(banks)
            for i, bank in enumerate(banks):
                nc.scalar.copy(out=y[:, i * per_bank : (i + 1) * per_bank, :], in_=bank[:])
            nc.sync.dma_start(out=y_rows[:, :, cols], in_=y[:])
            y_b = keep.tile([P, width * PACK], BF16, name="y_b%d" % cols.start, align_bytes=64)
            interleave(nc.vector.tensor_copy, y_b[:], y[:])
            return y_b

        def score_planes(cols, y_b):
            quantise(y_b[:], y_c[:, cols], y_s[:, cols])
            nc.sync.dma_start(out=y_words[:, cols], in_=y_c[:, cols])

        rounded = []
        for i, cols in enumerate(chunks):
            rounded.append(scores(cols))
            if i >= 1:
                score_planes(chunks[i - 1], rounded[i - 1])
        score_planes(chunks[-1], rounded[-1])
        for q in range(QUADRANTS):
            (nc.sync if q < QUADRANTS // 2 else nc.scalar).dma_start(
                out=out_2[0, 4 * q : 4 * q + 4, :].bitcast(I32), in_=y_s[32 * q : 32 * q + 4, :].bitcast(I32)
            )
